import numpy as np
import ml_dtypes


def mxq(x, axis, fmt="e4m3"):
    dtype, down = {"e4m3": (ml_dtypes.float8_e4m3fn, 7), "e5m2": (ml_dtypes.float8_e5m2, 14)}[fmt]
    v = np.moveaxis(np.asarray(x, np.float32).astype(ml_dtypes.bfloat16).astype(np.float64), axis, -1)
    blocks = v.reshape(v.shape[:-1] + (-1, 32))
    amax = np.abs(blocks).max(-1, keepdims=True)
    byte = np.maximum(np.where(amax > 0, np.frexp(amax)[1] - 1 + 127, 0) - down, 1)
    scale = np.exp2(byte - 127.0)
    codes = (blocks / scale).astype(np.float32).astype(dtype).astype(np.float64)
    return np.moveaxis((codes * scale).reshape(v.shape), -1, axis)


WIDE = False


def mx_kscale(k):
    if not WIDE:
        return np.ones(k)
    levels = np.array([10, -10, 5, -5, 0])
    if k % 512:
        return np.exp2(np.random.permutation(np.resize(levels, k // 32))).repeat(32)
    a = np.empty((k // 512, 16))
    for p in range(k // 512):
        a[p, :8] = np.random.permutation(np.resize(levels, 8))
        for g in range(8):
            far = levels[np.abs(levels - a[p, g]) >= 10]
            a[p, g + 8] = far[np.random.randint(len(far))]
    return np.exp2(a.ravel()).repeat(32)


def f64(x):
    return np.asarray(x).astype(np.float64)


def striped(idx):
    return np.tile(idx.reshape(-1, 16).T, (8, 1)).astype(np.uint16)


def unstriped(offs):
    return offs[:16].T.reshape(-1).astype(np.int64)


E2M1 = np.array([0.0, 0.5, 1.0, 1.5, 2.0, 3.0, 4.0, 6.0, -0.0, -0.5, -1.0, -1.5, -2.0, -3.0, -4.0, -6.0])


def pack_weight(w, fmt):
    k, n = w.shape
    w = f64(np.asarray(w, np.float32).astype(ml_dtypes.bfloat16)).reshape(k // 32, 32, n)
    amax = np.abs(w).max(1)
    if fmt == "e4m3":
        byte = np.frexp(amax)[1] - 1 + 127 - 7
    else:
        mant, ex = np.frexp(amax / 6.0)
        byte = np.where(mant > 0.5, ex, ex - 1) + 127
    byte = np.clip(np.where(amax > 0, byte, 1), 1, 254)
    scaled = (w * np.exp2(127.0 - byte)[:, None, :]).reshape(k, n).astype(np.float32)
    by_word = np.ascontiguousarray(scaled.reshape(k // 512, 128, 4, n).transpose(0, 1, 3, 2))
    if fmt == "e4m3":
        words = by_word.astype(ml_dtypes.float8_e4m3fn).view(np.uint8)
    else:
        c = by_word.astype(ml_dtypes.float4_e2m1fn).view(np.uint8) & 0xF
        words = (c[..., 0::2] | (c[..., 1::2] << 4)).reshape(k // 512, 128, 2 * n)
    return np.ascontiguousarray(words), np.ascontiguousarray(byte.astype(np.uint8).reshape(k // 512, 16, n))


def unpack_weight(words, scales, fmt):
    g, _, n = scales.shape
    words = np.ascontiguousarray(words).reshape(g, 128, n, -1)
    if fmt == "e4m3":
        vals = words.view(ml_dtypes.float8_e4m3fn).astype(np.float64)
    else:
        nib = np.empty((g, 128, n, 4), np.uint8)
        nib[..., 0::2] = words & 0xF
        nib[..., 1::2] = words >> 4
        vals = E2M1[nib]
    vals = vals * np.repeat(np.exp2(scales.astype(np.float64) - 127.0), 8, axis=1)[..., None]
    return vals.transpose(0, 1, 3, 2).reshape(g * 512, n)


def gelu(v):
    return 0.5 * v * (1.0 + np.tanh(np.sqrt(2.0 / np.pi) * (v + 0.044715 * v**3)))


def bf(x):
    return np.asarray(x, np.float32).astype(ml_dtypes.bfloat16)


def planes(Y):
    n, m = Y.shape
    b = f64(bf(Y)).reshape(n // 32, 32, m)
    amax = np.abs(b).max(1)
    byte = np.clip(np.where(amax > 0, np.frexp(amax)[1] - 1 + 127 - 7, 1), 1, 254)
    codes = (b * np.exp2(127.0 - byte)[:, None, :]).reshape(n, m).astype(np.float32).astype(ml_dtypes.float8_e4m3fn).view(np.uint8)
    words = codes.reshape(n // 512, 128, 4, m).transpose(0, 1, 3, 2)
    return np.ascontiguousarray(words), np.ascontiguousarray(byte.astype(np.uint8).reshape(n // 512, 16, m))


K, H, N, T, S, T2, P = 1536, 1024, 512, 2048, 1024, 2048, 512

def setup_inputs():
    n = np.random.standard_normal
    s = mx_kscale(K)[:, None]
    u = mx_kscale(H)[:, None]
    d = {}
    d["tab_words"], d["tab_scales"] = pack_weight(n((K, T)) * s, "e4m3")
    d["offs"] = striped(np.random.permutation(T)[:S])
    d["w1"] = (1.3 * n((K, H)) / s / K ** 0.5).astype(np.float32)
    d["b1"] = (0.7 * n(H)).astype(np.float32)
    d["gain"] = (1.5 * np.exp(0.3 * n(H)) * u[:, 0]).astype(np.float32)
    d["page0"] = (n((H, T2)) * u).astype(np.float32)
    d["wgs"] = np.exp(0.3 * n((128, S))).astype(np.float32)
    d["offs2"] = striped(np.random.permutation(T2)[:S])
    d["offs3"] = striped(np.random.permutation(T2)[:P])
    d["cap"] = (0.9 * np.exp(0.3 * n(H)) * u[:, 0]).astype(np.float32)
    d["w4_words"], d["w4_scales"] = pack_weight(n((H, N)) / u / H ** 0.5, "e2m1")
    d["solvent"] = (0.6 * n((N, P))).astype(np.float32)
    return d

def reference(tab_words, tab_scales, offs, w1, b1, gain, page0, wgs, offs2, offs3, cap, w4_words, w4_scales, solvent):
    v = unpack_weight(tab_words, tab_scales, "e4m3")[:, unstriped(offs)]
    f = (mxq(f64(w1), 0, "e4m3").T @ v) + f64(b1)[:, None]
    h = f64(gain)[:, None] * (f / (1.0 + np.exp(-f)))
    page = f64(page0).copy()
    page[:, unstriped(offs2)] = np.tile(f64(wgs), (H // 128, 1)) * h
    x = np.minimum(page[:, unstriped(offs3)], f64(cap)[:, None])
    w4 = unpack_weight(w4_words, w4_scales, "e2m1")
    y = (w4.T @ mxq(x, 0, "e4m3")) - f64(solvent)
    words, scales = planes(page)
    return y, page, words, scales

@@ -1,0 +1,373 @@
+from contextlib import ExitStack
+
+import concourse.mybir as mybir
+from concourse.masks import make_identity
+
+K, H, N, T, S, T2, PICKS = 1536, 1024, 512, 2048, 1024, 2048, 512
+FLOPS = 2 * K * H * S + 2 * H * N * PICKS
+
+F32 = mybir.dt.float32
+BF16 = mybir.dt.bfloat16
+I32 = mybir.dt.int32
+U32 = mybir.dt.uint32
+U16 = mybir.dt.uint16
+U8 = mybir.dt.uint8
+FP8X4 = mybir.dt.float8_e4m3fn_x4
+FP4X4 = mybir.dt.float4_e2m1fn_x4
+ACT = mybir.ActivationFunctionType
+ALU = mybir.AluOpType
+
+P = 128
+BANK = 512
+K_PASSES = K // 512
+SLICES = H // P
+GROUPS = H // 512
+RAW = K_PASSES * 4 * P
+HALVED = 3
+
+
+def tile_list_cork_taint_page_kernel(
+    tc, tab_words, tab_scales, offs, w1, b1, gain, page0, wgs, offs2, offs3, cap,
+    w4_words, w4_scales, solvent, out_0, out_1, out_2, out_3,
+):
+    nc = tc.nc
+    with ExitStack() as ctx:
+        sb = ctx.enter_context(tc.tile_pool(name="sb", bufs=1))
+        ps = ctx.enter_context(tc.psum_pool(name="ps", bufs=1))
+
+        banks = [ps.tile([P, BANK], F32, name=f"bank{b}") for b in range(8)]
+
+        idx = sb.tile([P, S // 16], U16, name="idx")
+        idx2 = sb.tile([P, S // 16], U16, name="idx2")
+        idx3 = sb.tile([P, PICKS // 16], U16, name="idx3")
+        tab_sc = sb.tile([P, T], U8, name="tab_sc", align_bytes=64)
+        tab_w = sb.tile([P, K_PASSES * T], I32, name="tab_w", tag="big", align_bytes=64)
+        got_w = sb.tile([P, K_PASSES * S], U32, name="got_w", align_bytes=64)
+        got_sc = sb.tile([P, S], U8, name="got_sc", align_bytes=64)
+        raw_low = [sb.tile([P, RAW], F32, name=f"raw{i}", tag=f"raw{i}", align_bytes=64) for i in range(4)]
+        w_bf = [sb.tile([P, RAW], BF16, name=f"w_bf{i}", align_bytes=64) for i in range(3)]
+        w_codes = [sb.tile([P, K_PASSES * P], U32, name=f"w_codes{i}", align_bytes=64) for i in range(3)]
+        w_sc = [sb.tile([P, K_PASSES * P], U8, name=f"w_sc{i}", align_bytes=64) for i in range(3)]
+        page = [sb.tile([P, T2], F32, name=f"page{i}") for i in range(SLICES)]
+        wgs_sb = sb.tile([P, S], F32, name="wgs_sb")
+        ident = sb.tile([P, P], F32, name="ident")
+        vec_rows = sb.tile([P, P], F32, name="vec_rows")
+        cap_rows = sb.tile([P, P], F32, name="cap_rows")
+        vecs = sb.tile([P, 2 * SLICES], F32, name="vecs")
+        caps = sb.tile([P, SLICES], F32, name="caps")
+        warm = sb.tile([P, 1], F32, name="warm")
+        wg_low = [sb.tile([P, S], F32, name=f"wg{i}", tag=f"turned{i}") for i in range(4)]
+        wg_mid = sb.tile([P, 2 * S], F32, name="wg_mid", tag="page_bf0", align_bytes=64)
+        wg_six = sb.tile([P, S], F32, name="wg_six", tag="x_t1")
+        wg = [t[:] for t in wg_low] + [wg_mid[:, :S], wg_mid[:, S:], wg_six[:], wgs_sb[:]]
+        page_t = [[sb.tile([P, 4 * 512], BF16, name=f"page_t0_{c}") for c in range(4)]]
+        page_codes = [sb.tile([P, T2], U32, name=f"page_codes{g}", align_bytes=64) for g in range(GROUPS)]
+        page_sc = [sb.tile([P, T2], U8, name=f"page_sc{g}", align_bytes=64) for g in range(GROUPS)]
+        x_codes = [sb.tile([P, PICKS], U32, name=f"x_codes{g}", align_bytes=64) for g in range(GROUPS)]
+        x_sc = [sb.tile([P, PICKS], U8, name=f"x_sc{g}", align_bytes=64) for g in range(GROUPS)]
+        w4_w = sb.tile([P, GROUPS * 2 * N], U8, name="w4_w", align_bytes=64)
+        w4_sc = sb.tile([P, GROUPS * N], U8, name="w4_sc", align_bytes=64)
+        y_sb = sb.tile([P, N // P, PICKS], F32, name="y_sb")
+
+        raw = [t[:] for t in raw_low]
+
+        def load_w1(i):
+            for a in range(K_PASSES):
+                nc.sync.dma_start(
+                    out=raw[i][:, 512 * a : 512 * (a + 1)].rearrange("p (j c) -> p j c", j=4),
+                    in_=w1[512 * a : 512 * (a + 1), P * i : P * (i + 1)].rearrange("(p j) c -> p j c", j=4),
+                )
+
+        def load_words(a):
+            nc.sync.dma_start(
+                out=tab_w[:, T * a : T * (a + 1)],
+                in_=tab_words[a].rearrange("p t i -> p (t i)").bitcast(I32),
+            )
+
+        def load_page(i):
+            nc.sync.dma_start(out=page[i][:], in_=page0[P * i : P * (i + 1), :])
+
+        nc.gpsimd.memset(vec_rows[:], 0.0)
+        nc.gpsimd.memset(tab_sc[:].bitcast(I32), 0)
+        make_identity(nc, ident[:])
+        nc.gpsimd.memset(cap_rows[:], 0.0)
+        nc.gpsimd.memset(w4_sc[:].bitcast(I32), 0)
+
+        nc.sync.dma_start(idx[:], offs)
+        load_words(0)
+        for v, vec in enumerate((gain, b1)):
+            nc.scalar.dma_start(out=vec_rows[SLICES * v : SLICES * (v + 1), :], in_=vec.rearrange("(i p) -> i p", p=P))
+        for q in range(4):
+            nc.scalar.dma_start(
+                out=tab_sc[32 * q : 32 * q + 4 * K_PASSES, :].bitcast(I32),
+                in_=tab_scales[:, 4 * q : 4 * q + 4, :].bitcast(I32),
+            )
+        nc.scalar.activation(out=warm[:], in_=ident[:, :1], func=ACT.Silu)
+        nc.sync.dma_start(out=wgs_sb[:], in_=wgs)
+        load_words(1)
+        load_w1(0)
+        load_words(2)
+        load_page(0)
+        nc.sync.dma_start(idx2[:], offs2)
+        load_w1(1)
+        load_w1(2)
+        load_page(1)
+        load_w1(3)
+
+        nc.tensor.transpose(banks[6][:, :P], vec_rows[:], ident[:])
+        nc.scalar.copy(out=vecs[:], in_=banks[6][:, : 2 * SLICES])
+
+        def weigh(i):
+            nc.scalar.activation(out=wg[i], in_=wgs_sb[:], func=ACT.Copy, scale=vecs[:, i : i + 1])
+
+        def quantize_w1(i):
+            staged, codes, scales = w_bf[i % 3], w_codes[i % 3], w_sc[i % 3]
+            for a in range(K_PASSES):
+                cols = slice(512 * a, 512 * (a + 1))
+                nc.scalar.copy(
+                    out=staged[:, cols].rearrange("p (c n j) -> p c j n", n=4, j=4),
+                    in_=raw[i][:, cols].rearrange("p (j c n) -> p c j n", n=4, j=4),
+                )
+            for first, last in ((0, 1), (1, 2), (2, 3)) if i == 0 else ((0, 2), (2, 3)):
+                nc.vector.quantize_mx(
+                    out=codes[:, P * first : P * last].bitcast(FP8X4),
+                    scales=scales[:, P * first : P * last],
+                    in_=staged[:, 512 * first : 512 * last],
+                )
+
+        def gather_words(a, first, count):
+            nc.vector.tensor_copy(
+                out=got_w[:, S * a + first : S * a + first + count],
+                in_=tab_w[:, T * a : T * (a + 1)].bitcast(U32).indirect(idx[:, first // 16 : (first + count) // 16]),
+            )
+
+        gather_words(0, 0, S)
+        nc.vector.tensor_copy(out=got_sc[:], in_=tab_sc[:].indirect(idx[:]))
+        weigh(0)
+        gather_words(1, 0, S)
+        quantize_w1(0)
+        gather_words(2, 0, S // 2)
+        gather_words(2, S // 2, S // 2)
+
+        raw_high = sb.tile([P, 4 * RAW], F32, name="raw_high", tag="big", align_bytes=64)
+        raw.extend(raw_high[:, RAW * i : RAW * (i + 1)] for i in range(4))
+        for i in range(4, SLICES):
+            load_w1(i)
+            load_page(i - 2)
+        for i in range(SLICES - 2, SLICES):
+            load_page(i)
+        nc.sync.dma_start(idx3[:], offs3)
+        nc.sync.dma_start(out=cap_rows[:SLICES, :], in_=cap.rearrange("(i p) -> i p", p=P))
+        nc.sync.dma_start(out=y_sb[:], in_=solvent.rearrange("(t p) j -> p t j", p=P))
+        nc.sync.dma_start(
+            out=w4_w[:].bitcast(I32).rearrange("p (g c) -> p g c", g=GROUPS),
+            in_=w4_words.bitcast(I32).rearrange("g p c -> p g c"),
+        )
+        for q in range(4):
+            nc.sync.dma_start(
+                out=w4_sc[32 * q : 32 * q + 4, :].bitcast(I32).rearrange("r (g c) -> r g c", g=GROUPS),
+                in_=w4_scales[:, 4 * q : 4 * q + 4, :].bitcast(I32).rearrange("g r c -> r g c"),
+            )
+
+        def feature_banks(i):
+            return banks[2 * (i % 2)], banks[2 * (i % 2) + 1]
+
+        def h_home(i):
+            return i + 2 if i + 2 < SLICES else SLICES - 1 - i
+
+        def h_half(i, half):
+            if i < HALVED:
+                home, slot = ((0, 0), (1, 0), (1, 1), (2, 0), (3, 0), (4, 0))[2 * i + half]
+            else:
+                home, slot = h_home(i), 1 + half
+            return raw[home][:, BANK * slot : BANK * (slot + 1)]
+
+        def multiply_w1(i):
+            codes, scales = w_codes[i % 3], w_sc[i % 3]
+            for a in range(K_PASSES):
+                for half in range(2):
+                    cols = slice(BANK * half, BANK * (half + 1))
+                    nc.tensor.matmul_mx(
+                        out=feature_banks(i)[half][:],
+                        lhsT=codes[:, P * a : P * (a + 1)].bitcast(FP8X4),
+                        lhsT_scale=scales[:, P * a : P * (a + 1)],
+                        rhs=got_w[:, S * a + BANK * half : S * a + BANK * (half + 1)].bitcast(FP8X4),
+                        rhs_scale=got_sc[4 * a : P, cols],
+                        start=(a == 0),
+                        stop=(a == K_PASSES - 1),
+                    )
+
+        def activate(i, halves):
+            for half in halves:
+                nc.scalar.activation(
+                    out=h_half(i, half), in_=feature_banks(i)[half][:], func=ACT.Silu, bias=vecs[:, SLICES + i : SLICES + i + 1]
+                )
+
+        def scatter_half(i, half):
+            nc.vector.tensor_tensor(
+                page[i][:].indirect(idx2[:, 32 * half : 32 * (half + 1)]),
+                h_half(i, half), wg[i][:, BANK * half : BANK * (half + 1)], ALU.mult,
+            )
+
+        def scatter_whole(i):
+            nc.vector.tensor_tensor(
+                page[i][:].indirect(idx2[:]), raw[h_home(i)][:, BANK:], wg[i], ALU.mult
+            )
+
+        def turn(src, dst, il, bank):
+            for b in range(4):
+                nc.tensor.transpose(bank[:, P * b : P * (b + 1)], src[:, P * b : P * (b + 1)], ident[:])
+            nc.scalar.copy(
+                out=dst.rearrange("m (b u l p e) -> m b u l p e", b=4, u=2, l=4, e=2)[:, :, :, il],
+                in_=bank[:].rearrange("m (b p u e) -> m b u p e", b=4, u=2, e=2),
+            )
+
+        def turn_back(src, dst, bank):
+            words = src.bitcast(F32)
+            for k in range(4):
+                nc.tensor.transpose(bank[:, P * k : P * (k + 1)], words[:, P * k : P * (k + 1)], ident[:])
+            nc.scalar.copy(
+                out=dst.bitcast(F32).rearrange("p (b m u) -> p b m u", b=2, u=2),
+                in_=bank[:].rearrange("p (b u m) -> p b m u", b=2, u=2),
+            )
+
+        def turn_page(i):
+            for c in range(4):
+                turn(page[i][:, 512 * c : 512 * (c + 1)], page_t[i // 4][c][:], i % 4, feature_banks(i + 1)[1 - c % 2])
+
+        page_bf = []
+
+        def turn_page_back(g, job, bank):
+            turn_back(page_t[g][job // 2][:, 1024 * (job % 2) : 1024 * (job % 2 + 1)],
+                      page_bf[g][:, 1024 * job : 1024 * (job + 1)], bank)
+
+        def quantize_page(g, c):
+            nc.vector.quantize_mx(
+                out=page_codes[g][:, 512 * c : 512 * (c + 1)].bitcast(FP8X4),
+                scales=page_sc[g][:, 512 * c : 512 * (c + 1)],
+                in_=page_bf[g][:, 2048 * c : 2048 * (c + 1)],
+            )
+
+        def store_page(i):
+            nc.sync.dma_start(out=out_1[P * i : P * (i + 1), :], in_=page[i][:])
+
+        def store_codes(g, first, count):
+            nc.sync.dma_start(
+                out=out_2[g, :, first : first + count, :].rearrange("p m t -> p (m t)").bitcast(I32),
+                in_=page_codes[g][:, first : first + count].bitcast(I32),
+            )
+
+        def store_scales(g):
+            for q in range(4):
+                nc.sync.dma_start(
+                    out=out_3[g, 4 * q : 4 * q + 4, :].bitcast(I32),
+                    in_=page_sc[g][32 * q : 32 * q + 4, :].bitcast(I32),
+                )
+
+        multiply_w1(0)
+        for i in range(SLICES):
+            if i < HALVED:
+                if i == HALVED - 1:
+                    quantize_w1(i + 1)
+                activate(i, (0,))
+                scatter_half(i, 0)
+                quantize_w1(i + 2 if i == HALVED - 1 else i + 1)
+                activate(i, (1,))
+                scatter_half(i, 1)
+            else:
+                if i + 2 < SLICES:
+                    quantize_w1(i + 2)
+                activate(i, (0, 1))
+                scatter_whole(i)
+            if i == 0:
+                for later in range(1, SLICES):
+                    weigh(later)
+            if i + 1 < SLICES:
+                multiply_w1(i + 1)
+            store_page(i)
+            if i == 4:
+                page_t.append([sb.tile([P, 4 * 512], BF16, name=f"page_t1_{c}", tag=f"turned{c}") for c in range(4)])
+            if i == SLICES - 1:
+                page_bf.append(sb.tile([P, 4 * T2], BF16, name="page_bf0", tag="page_bf0", align_bytes=64))
+                for job in range(4):
+                    turn_page_back(0, job, feature_banks(0)[job % 2])
+            if i >= 1:
+                turn_page(i - 1)
+            if i == SLICES - 1:
+                for job in range(4, 8):
+                    turn_page_back(0, job, feature_banks(0)[job % 2])
+        nc.tensor.transpose(banks[7][:, :P], cap_rows[:], ident[:])
+        nc.scalar.copy(out=caps[:], in_=banks[7][:, :SLICES])
+        turn_page(SLICES - 1)
+
+        page_bf.append(sb.tile([P, 4 * T2], BF16, name="page_bf1", tag="big", align_bytes=64))
+        x_t = [
+            sb.tile([P, 4 * 512], BF16, name="x_t0", tag="raw3", align_bytes=64),
+            sb.tile([P, 4 * 512], BF16, name="x_t1", tag="x_t1"),
+        ]
+        x_bf = [sb.tile([P, 4 * PICKS], BF16, name=f"x_bf{g}", tag=f"raw{1 + g}", align_bytes=64) for g in range(GROUPS)]
+        picked = [raw[0][:, BANK : 2 * BANK], raw[0][:, 2 * BANK :], wgs_sb[:, :BANK], wgs_sb[:, BANK:]]
+
+        def pick(i):
+            nc.vector.tensor_copy(out=picked[i % 4], in_=page[i][:].indirect(idx3[:]))
+
+        def cap_pick(i):
+            nc.vector.tensor_scalar(
+                out=picked[i % 4], in0=picked[i % 4], scalar1=caps[:, i : i + 1],
+                scalar2=None, op0=ALU.min,
+            )
+
+        def quantize_x(g):
+            nc.vector.quantize_mx(out=x_codes[g][:].bitcast(FP8X4), scales=x_sc[g][:], in_=x_bf[g][:])
+
+        def multiply_w4(g):
+            for t in range(N // P):
+                first = N * g + P * t
+                nc.tensor.matmul_mx(
+                    out=banks[4 + t][:],
+                    lhsT=w4_w[:, 2 * first : 2 * (first + P)].bitcast(FP4X4),
+                    lhsT_scale=w4_sc[:, first : first + P],
+                    rhs=x_codes[g][:].bitcast(FP8X4),
+                    rhs_scale=x_sc[g][:],
+                    start=(g == 0),
+                    stop=(g == GROUPS - 1),
+                )
+
+        ring = []
+
+        def ring_bank():
+            ring.append(banks[(len(ring) + 2) % 4])
+            return ring[-1]
+
+        pick(0)
+        for i in range(SLICES):
+            if i + 1 < SLICES:
+                pick(i + 1)
+            cap_pick(i)
+            if i < 4:
+                quantize_page(0, i)
+            if i >= 1:
+                turn_page_back(1, i - 1, ring_bank())
+            turn(picked[i % 4], x_t[i // 4][:], i % 4, ring_bank())
+            if i == 3:
+                store_codes(0, 0, T2)
+                store_scales(0)
+            if i == 4:
+                for job in range(2):
+                    turn_back(x_t[0][:, 1024 * job : 1024 * (job + 1)], x_bf[0][:, 1024 * job : 1024 * (job + 1)], ring_bank())
+        turn_page_back(1, 7, ring_bank())
+        for job in range(2):
+            turn_back(x_t[1][:, 1024 * job : 1024 * (job + 1)], x_bf[1][:, 1024 * job : 1024 * (job + 1)], ring_bank())
+        for c in range(3):
+            quantize_page(1, c)
+            store_codes(1, 512 * c, 512)
+        quantize_x(0)
+        multiply_w4(0)
+        quantize_x(1)
+        multiply_w4(1)
+        quantize_page(1, 3)
+        store_codes(1, 512 * 3, 512)
+        store_scales(1)
+        for t in range(N // P):
+            nc.vector.tensor_tensor(y_sb[:, t, :], banks[4 + t][:], y_sb[:, t, :], ALU.subtract)
+            nc.sync.dma_start(out=out_0[P * t : P * (t + 1), :], in_=y_sb[:, t, :])

@@ -18,12 +18,20 @@ ACT = mybir.ActivationFunctionType
 ALU = mybir.AluOpType
 
 P = 128
+PASS = 4 * P
 BANK = 512
-K_PASSES = K // 512
+K_PASSES = K // PASS
 SLICES = H // P
-GROUPS = H // 512
-RAW = K_PASSES * 4 * P
+GROUPS = H // PASS
+PER_GROUP = SLICES // GROUPS
+RAW = K_PASSES * PASS
+HALF = S // 2
+QUARTER = S // 4
+CHUNK = T2 // 4
+BACK = 2 * PASS
+W_TILES = 3
 HALVED = 3
+LOW_BACK_JOBS = ((0, 2), (2, 5), (5, 8))
 
 
 def tile_list_cork_taint_page_kernel(
@@ -44,25 +52,25 @@ def tile_list_cork_taint_page_kernel(
         tab_w = sb.tile([P, K_PASSES * T], I32, name="tab_w", tag="big", align_bytes=64)
         got_w = sb.tile([P, K_PASSES * S], U32, name="got_w", align_bytes=64)
         got_sc = sb.tile([P, S], U8, name="got_sc", align_bytes=64)
-        raw_low = [sb.tile([P, RAW], F32, name=f"raw{i}", tag=f"raw{i}", align_bytes=64) for i in range(4)]
-        w_bf = [sb.tile([P, RAW], BF16, name=f"w_bf{i}", align_bytes=64) for i in range(3)]
-        w_codes = [sb.tile([P, K_PASSES * P], U32, name=f"w_codes{i}", align_bytes=64) for i in range(3)]
-        w_sc = [sb.tile([P, K_PASSES * P], U8, name=f"w_sc{i}", align_bytes=64) for i in range(3)]
-        page = [sb.tile([P, T2], F32, name=f"page{i}") for i in range(SLICES)]
+        raw_low = [sb.tile([P, RAW], F32, name=f"raw{i}", tag=f"raw{i}", align_bytes=64) for i in range(PER_GROUP)]
+        w_bf = [sb.tile([P, RAW], BF16, name=f"w_bf{i}", align_bytes=64) for i in range(W_TILES)]
+        w_codes = [sb.tile([P, K_PASSES * P], U32, name=f"w_codes{i}", align_bytes=64) for i in range(W_TILES)]
+        w_sc = [sb.tile([P, K_PASSES * P], U8, name=f"w_sc{i}", align_bytes=64) for i in range(W_TILES)]
+        page = [sb.tile([P, T2], F32, name=f"page{i}", tag=f"page{i}", align_bytes=64) for i in range(SLICES)]
         wgs_sb = sb.tile([P, S], F32, name="wgs_sb")
         ident = sb.tile([P, P], F32, name="ident")
         vec_rows = sb.tile([P, P], F32, name="vec_rows")
+        vec_in = sb.tile([2 * SLICES, P], F32, name="vec_in")
         cap_rows = sb.tile([P, P], F32, name="cap_rows")
         vecs = sb.tile([P, 2 * SLICES], F32, name="vecs")
         caps = sb.tile([P, SLICES], F32, name="caps")
-        warm = sb.tile([P, 1], F32, name="warm")
-        wg_low = [sb.tile([P, S], F32, name=f"wg{i}", tag=f"turned{i}") for i in range(4)]
-        wg_mid = sb.tile([P, 2 * S], F32, name="wg_mid", tag="page_bf0", align_bytes=64)
-        wg_six = sb.tile([P, S], F32, name="wg_six", tag="x_t1")
-        wg = [t[:] for t in wg_low] + [wg_mid[:, :S], wg_mid[:, S:], wg_six[:], wgs_sb[:]]
-        page_t = [[sb.tile([P, 4 * 512], BF16, name=f"page_t0_{c}") for c in range(4)]]
-        page_codes = [sb.tile([P, T2], U32, name=f"page_codes{g}", align_bytes=64) for g in range(GROUPS)]
-        page_sc = [sb.tile([P, T2], U8, name=f"page_sc{g}", align_bytes=64) for g in range(GROUPS)]
+        wg_single = [sb.tile([P, S], F32, name=f"wg{i}", tag=f"wg{i}", align_bytes=64) for i in range(SLICES - 3)]
+        wg_pair = sb.tile([P, 2 * S], F32, name="wg_pair", tag="wg_pair", align_bytes=64)
+        wg = wg_single + [wg_pair[:, :S], wg_pair[:, S:], wgs_sb]
+        group_t = [sb.tile([P, T2], BF16, name=f"group_t{c}") for c in range(T2 // CHUNK)]
+        slice_bf = [sb.tile([P, T2], BF16, name=f"slice_bf{i}", align_bytes=64) for i in range(2)]
+        high_sc = sb.tile([P, T2], U8, name="high_sc", align_bytes=64)
+        low_sc = sb.tile([P, T2], U8, name="low_sc", align_bytes=64)
         x_codes = [sb.tile([P, PICKS], U32, name=f"x_codes{g}", align_bytes=64) for g in range(GROUPS)]
         x_sc = [sb.tile([P, PICKS], U8, name=f"x_sc{g}", align_bytes=64) for g in range(GROUPS)]
         w4_w = sb.tile([P, GROUPS * 2 * N], U8, name="w4_w", align_bytes=64)
@@ -74,8 +82,8 @@ def tile_list_cork_taint_page_kernel(
         def load_w1(i):
             for a in range(K_PASSES):
                 nc.sync.dma_start(
-                    out=raw[i][:, 512 * a : 512 * (a + 1)].rearrange("p (j c) -> p j c", j=4),
-                    in_=w1[512 * a : 512 * (a + 1), P * i : P * (i + 1)].rearrange("(p j) c -> p j c", j=4),
+                    out=raw[i][:, PASS * a : PASS * (a + 1)].rearrange("p (j c) -> p j c", j=4),
+                    in_=w1[PASS * a : PASS * (a + 1), P * i : P * (i + 1)].rearrange("(p j) c -> p j c", j=4),
                 )
 
         def load_words(a):
@@ -87,8 +95,8 @@ def tile_list_cork_taint_page_kernel(
         def load_page(i):
             nc.sync.dma_start(out=page[i][:], in_=page0[P * i : P * (i + 1), :])
 
-        nc.gpsimd.memset(vec_rows[:], 0.0)
         nc.gpsimd.memset(tab_sc[:].bitcast(I32), 0)
+        nc.gpsimd.memset(vec_rows[:], 0.0)
         make_identity(nc, ident[:])
         nc.gpsimd.memset(cap_rows[:], 0.0)
         nc.gpsimd.memset(w4_sc[:].bitcast(I32), 0)
@@ -96,13 +104,12 @@ def tile_list_cork_taint_page_kernel(
         nc.sync.dma_start(idx[:], offs)
         load_words(0)
         for v, vec in enumerate((gain, b1)):
-            nc.scalar.dma_start(out=vec_rows[SLICES * v : SLICES * (v + 1), :], in_=vec.rearrange("(i p) -> i p", p=P))
+            nc.sync.dma_start(out=vec_in[SLICES * v : SLICES * (v + 1), :], in_=vec.rearrange("(i p) -> i p", p=P))
         for q in range(4):
             nc.scalar.dma_start(
                 out=tab_sc[32 * q : 32 * q + 4 * K_PASSES, :].bitcast(I32),
                 in_=tab_scales[:, 4 * q : 4 * q + 4, :].bitcast(I32),
             )
-        nc.scalar.activation(out=warm[:], in_=ident[:, :1], func=ACT.Silu)
         nc.sync.dma_start(out=wgs_sb[:], in_=wgs)
         load_words(1)
         load_w1(0)
@@ -110,20 +117,23 @@ def tile_list_cork_taint_page_kernel(
         load_page(0)
         nc.sync.dma_start(idx2[:], offs2)
         load_w1(1)
-        load_w1(2)
+        nc.sync.dma_start(out=cap_rows[:SLICES, :], in_=cap.rearrange("(i p) -> i p", p=P))
         load_page(1)
+        load_w1(2)
         load_w1(3)
+        load_page(2)
 
-        nc.tensor.transpose(banks[6][:, :P], vec_rows[:], ident[:])
-        nc.scalar.copy(out=vecs[:], in_=banks[6][:, : 2 * SLICES])
+        nc.gpsimd.tensor_copy(out=vec_rows[: 2 * SLICES, :], in_=vec_in[:])
+        nc.tensor.transpose(banks[7][:, :P], vec_rows[:], ident[:])
+        nc.scalar.copy(out=vecs[:], in_=banks[7][:, : 2 * SLICES])
 
         def weigh(i):
-            nc.scalar.activation(out=wg[i], in_=wgs_sb[:], func=ACT.Copy, scale=vecs[:, i : i + 1])
+            nc.scalar.activation(out=wg[i][:], in_=wgs_sb[:], func=ACT.Copy, scale=vecs[:, i : i + 1])
 
         def quantize_w1(i):
-            staged, codes, scales = w_bf[i % 3], w_codes[i % 3], w_sc[i % 3]
+            staged, codes, scales = w_bf[i % W_TILES], w_codes[i % W_TILES], w_sc[i % W_TILES]
             for a in range(K_PASSES):
-                cols = slice(512 * a, 512 * (a + 1))
+                cols = slice(PASS * a, PASS * (a + 1))
                 nc.scalar.copy(
                     out=staged[:, cols].rearrange("p (c n j) -> p c j n", n=4, j=4),
                     in_=raw[i][:, cols].rearrange("p (j c n) -> p c j n", n=4, j=4),
@@ -132,7 +142,7 @@ def tile_list_cork_taint_page_kernel(
                 nc.vector.quantize_mx(
                     out=codes[:, P * first : P * last].bitcast(FP8X4),
                     scales=scales[:, P * first : P * last],
-                    in_=staged[:, 512 * first : 512 * last],
+                    in_=staged[:, PASS * first : PASS * last],
                 )
 
         def gather_words(a, first, count):
@@ -144,20 +154,21 @@ def tile_list_cork_taint_page_kernel(
         gather_words(0, 0, S)
         nc.vector.tensor_copy(out=got_sc[:], in_=tab_sc[:].indirect(idx[:]))
         weigh(0)
-        gather_words(1, 0, S)
+        gather_words(1, 0, HALF)
         quantize_w1(0)
-        gather_words(2, 0, S // 2)
-        gather_words(2, S // 2, S // 2)
+        gather_words(2, 0, HALF)
+        gather_words(1, HALF, HALF)
+        gather_words(2, HALF, HALF)
 
-        raw_high = sb.tile([P, 4 * RAW], F32, name="raw_high", tag="big", align_bytes=64)
-        raw.extend(raw_high[:, RAW * i : RAW * (i + 1)] for i in range(4))
-        for i in range(4, SLICES):
+        raw_high = sb.tile([P, PER_GROUP * RAW], F32, name="raw_high", tag="big", align_bytes=64)
+        raw.extend(raw_high[:, RAW * i : RAW * (i + 1)] for i in range(PER_GROUP))
+        load_w1(PER_GROUP)
+        for i in range(PER_GROUP + 1, SLICES):
             load_w1(i)
             load_page(i - 2)
         for i in range(SLICES - 2, SLICES):
             load_page(i)
         nc.sync.dma_start(idx3[:], offs3)
-        nc.sync.dma_start(out=cap_rows[:SLICES, :], in_=cap.rearrange("(i p) -> i p", p=P))
         nc.sync.dma_start(out=y_sb[:], in_=solvent.rearrange("(t p) j -> p t j", p=P))
         nc.sync.dma_start(
             out=w4_w[:].bitcast(I32).rearrange("p (g c) -> p g c", g=GROUPS),
@@ -170,56 +181,59 @@ def tile_list_cork_taint_page_kernel(
             )
 
         def feature_banks(i):
-            return banks[2 * (i % 2)], banks[2 * (i % 2) + 1]
+            return banks[4 * (i % 2) : 4 * (i % 2) + 4]
 
         def h_home(i):
             return i + 2 if i + 2 < SLICES else SLICES - 1 - i
 
         def h_half(i, half):
             if i < HALVED:
-                home, slot = ((0, 0), (1, 0), (1, 1), (2, 0), (3, 0), (4, 0))[2 * i + half]
+                home, third = ((0, 0), (1, 0), (1, 1), (2, 0), (3, 0), (4, 0))[2 * i + half]
             else:
-                home, slot = h_home(i), 1 + half
-            return raw[home][:, BANK * slot : BANK * (slot + 1)]
+                home, third = h_home(i), 1 + half
+            return raw[home][:, HALF * third : HALF * (third + 1)]
 
         def multiply_w1(i):
-            codes, scales = w_codes[i % 3], w_sc[i % 3]
-            for a in range(K_PASSES):
-                for half in range(2):
-                    cols = slice(BANK * half, BANK * (half + 1))
+            codes, scales = w_codes[i % W_TILES], w_sc[i % W_TILES]
+            for quarter in range(4):
+                first = QUARTER * quarter
+                for a in range(K_PASSES):
                     nc.tensor.matmul_mx(
-                        out=feature_banks(i)[half][:],
+                        out=feature_banks(i)[quarter][:, :QUARTER],
                         lhsT=codes[:, P * a : P * (a + 1)].bitcast(FP8X4),
                         lhsT_scale=scales[:, P * a : P * (a + 1)],
-                        rhs=got_w[:, S * a + BANK * half : S * a + BANK * (half + 1)].bitcast(FP8X4),
-                        rhs_scale=got_sc[4 * a : P, cols],
+                        rhs=got_w[:, S * a + first : S * a + first + QUARTER].bitcast(FP8X4),
+                        rhs_scale=got_sc[4 * a : P, first : first + QUARTER],
                         start=(a == 0),
                         stop=(a == K_PASSES - 1),
                     )
 
         def activate(i, halves):
             for half in halves:
-                nc.scalar.activation(
-                    out=h_half(i, half), in_=feature_banks(i)[half][:], func=ACT.Silu, bias=vecs[:, SLICES + i : SLICES + i + 1]
-                )
+                for part in range(2):
+                    nc.scalar.activation(
+                        out=h_half(i, half)[:, QUARTER * part : QUARTER * (part + 1)],
+                        in_=feature_banks(i)[2 * half + part][:, :QUARTER],
+                        func=ACT.Silu,
+                        bias=vecs[:, SLICES + i : SLICES + i + 1],
+                    )
 
         def scatter_half(i, half):
             nc.vector.tensor_tensor(
-                page[i][:].indirect(idx2[:, 32 * half : 32 * (half + 1)]),
-                h_half(i, half), wg[i][:, BANK * half : BANK * (half + 1)], ALU.mult,
+                page[i][:].indirect(idx2[:, HALF // 16 * half : HALF // 16 * (half + 1)]),
+                h_half(i, half), wg[i][:, HALF * half : HALF * (half + 1)], ALU.mult,
             )
 
         def scatter_whole(i):
-            nc.vector.tensor_tensor(
-                page[i][:].indirect(idx2[:]), raw[h_home(i)][:, BANK:], wg[i], ALU.mult
-            )
+            nc.vector.tensor_tensor(page[i][:].indirect(idx2[:]), raw[h_home(i)][:, HALF:], wg[i][:], ALU.mult)
 
-        def turn(src, dst, il, bank):
-            for b in range(4):
+        def turn(src, dst, place, bank):
+            blocks = src.shape[1] // P
+            for b in range(blocks):
                 nc.tensor.transpose(bank[:, P * b : P * (b + 1)], src[:, P * b : P * (b + 1)], ident[:])
             nc.scalar.copy(
-                out=dst.rearrange("m (b u l p e) -> m b u l p e", b=4, u=2, l=4, e=2)[:, :, :, il],
-                in_=bank[:].rearrange("m (b p u e) -> m b u p e", b=4, u=2, e=2),
+                out=dst.rearrange("m (b u l p e) -> m b u l p e", b=blocks, u=2, l=PER_GROUP, e=2)[:, :, :, place],
+                in_=bank[:, : P * blocks].rearrange("m (b p u e) -> m b u p e", b=blocks, u=2, e=2),
             )
 
         def turn_back(src, dst, bank):
@@ -231,38 +245,42 @@ def tile_list_cork_taint_page_kernel(
                 in_=bank[:].rearrange("p (b u m) -> p b m u", b=2, u=2),
             )
 
-        def turn_page(i):
-            for c in range(4):
-                turn(page[i][:, 512 * c : 512 * (c + 1)], page_t[i // 4][c][:], i % 4, feature_banks(i + 1)[1 - c % 2])
+        used = [0] * (SLICES + 1)
 
-        page_bf = []
+        def next_bank(i):
+            used[i] = used[i] + 1
+            return feature_banks(i)[-used[i] % 4]
 
-        def turn_page_back(g, job, bank):
-            turn_back(page_t[g][job // 2][:, 1024 * (job % 2) : 1024 * (job % 2 + 1)],
-                      page_bf[g][:, 1024 * job : 1024 * (job + 1)], bank)
+        def turn_low(i):
+            for c in range(T2 // CHUNK):
+                turn(page[i][:, CHUNK * c : CHUNK * (c + 1)], group_t[c][:], i, next_bank(i + 1))
 
-        def quantize_page(g, c):
-            nc.vector.quantize_mx(
-                out=page_codes[g][:, 512 * c : 512 * (c + 1)].bitcast(FP8X4),
-                scales=page_sc[g][:, 512 * c : 512 * (c + 1)],
-                in_=page_bf[g][:, 2048 * c : 2048 * (c + 1)],
+        def turn_low_back(job, bank):
+            turn_back(
+                group_t[job // 2][:, BACK * (job % 2) : BACK * (job % 2 + 1)],
+                group_bf[:, BACK * job : BACK * (job + 1)], bank,
             )
 
-        def store_page(i):
-            nc.sync.dma_start(out=out_1[P * i : P * (i + 1), :], in_=page[i][:])
-
-        def store_codes(g, first, count):
-            nc.sync.dma_start(
-                out=out_2[g, :, first : first + count, :].rearrange("p m t -> p (m t)").bitcast(I32),
-                in_=page_codes[g][:, first : first + count].bitcast(I32),
-            )
-
-        def store_scales(g):
-            for q in range(4):
-                nc.sync.dma_start(
-                    out=out_3[g, 4 * q : 4 * q + 4, :].bitcast(I32),
-                    in_=page_sc[g][32 * q : 32 * q + 4, :].bitcast(I32),
+        def turn_high(i):
+            halves = [
+                sb.tile([P, BACK], BF16, name=f"slice_t{i}_{h}", tag=f"wg{2 * (i % 2) + h}", align_bytes=64)
+                for h in range(2)
+            ]
+            for s in range(CHUNK // P):
+                bank = next_bank(i + 1)
+                for b in range(T2 // CHUNK):
+                    first = CHUNK * b + P * s
+                    nc.tensor.transpose(bank[:, P * b : P * (b + 1)], page[i][:, first : first + P], ident[:])
+                nc.scalar.copy(
+                    out=halves[s // 2][:, PASS * (s % 2) : PASS * (s % 2 + 1)].rearrange("m (u w e) -> m u w e", u=2, e=2),
+                    in_=bank[:].rearrange("m (w u e) -> m u w e", u=2, e=2),
                 )
+            for job in range(2):
+                turn_back(halves[job][:], slice_bf[i % 2][:, BACK * job : BACK * (job + 1)], next_bank(i + 1))
+
+        def quantize_high(i):
+            cols = slice(CHUNK * (i % PER_GROUP), CHUNK * (i % PER_GROUP + 1))
+            nc.vector.quantize_mx(out=high_codes[:, cols].bitcast(FP8X4), scales=high_sc[:, cols], in_=slice_bf[i % 2][:])
 
         multiply_w1(0)
         for i in range(SLICES):
@@ -277,45 +295,65 @@ def tile_list_cork_taint_page_kernel(
             else:
                 if i + 2 < SLICES:
                     quantize_w1(i + 2)
-                activate(i, (0, 1))
+                    activate(i, (0, 1))
                 scatter_whole(i)
             if i == 0:
                 for later in range(1, SLICES):
                     weigh(later)
             if i + 1 < SLICES:
                 multiply_w1(i + 1)
-            store_page(i)
-            if i == 4:
-                page_t.append([sb.tile([P, 4 * 512], BF16, name=f"page_t1_{c}", tag=f"turned{c}") for c in range(4)])
-            if i == SLICES - 1:
-                page_bf.append(sb.tile([P, 4 * T2], BF16, name="page_bf0", tag="page_bf0", align_bytes=64))
-                for job in range(4):
-                    turn_page_back(0, job, feature_banks(0)[job % 2])
-            if i >= 1:
-                turn_page(i - 1)
-            if i == SLICES - 1:
-                for job in range(4, 8):
-                    turn_page_back(0, job, feature_banks(0)[job % 2])
-        nc.tensor.transpose(banks[7][:, :P], cap_rows[:], ident[:])
-        nc.scalar.copy(out=caps[:], in_=banks[7][:, :SLICES])
-        turn_page(SLICES - 1)
+            if i + 1 < SLICES <= i + 3:
+                activate(i + 1, (0, 1))
+            nc.sync.dma_start(out=out_1[P * i : P * (i + 1), :], in_=page[i][:])
+            if 1 <= i <= PER_GROUP:
+                turn_low(i - 1)
+            if i == PER_GROUP:
+                bank = next_bank(i)
+                nc.tensor.transpose(bank[:, :P], cap_rows[:], ident[:])
+                nc.scalar.copy(out=caps[:], in_=bank[:, :SLICES])
+            if i == PER_GROUP + 1:
+                group_bf = sb.tile([P, 4 * T2], BF16, name="group_bf", tag=f"wg{PER_GROUP}", align_bytes=64)
+            if i == PER_GROUP + 2:
+                high_codes = sb.tile([P, T2], U32, name="high_codes", tag="wg_pair", align_bytes=64)
+                quantize_high(PER_GROUP)
+            if i > PER_GROUP:
+                turn_high(i - 1)
+                if i >= PER_GROUP + 2:
+                    quantize_high(i - 1)
+                for job in range(*LOW_BACK_JOBS[i - PER_GROUP - 1]):
+                    turn_low_back(job, next_bank(i))
+        turn_high(SLICES - 1)
+        quantize_high(SLICES - 1)
+        for b in range(4):
+            nc.sync.dma_start(
+                out=out_3[1, :, CHUNK * b : CHUNK * (b + 1)].rearrange("(l q) m -> q l m", l=PER_GROUP).bitcast(I32),
+                in_=high_sc[32 * b : 32 * b + 4, :].bitcast(I32).rearrange("q (l m) -> q l m", l=PER_GROUP),
+            )
+        for b in (0, 2, 1, 3):
+            nc.sync.dma_start(
+                out=out_2[1, :, CHUNK * b : CHUNK * (b + 1), :]
+                .rearrange("(l p) m t -> p l (m t)", l=PER_GROUP)
+                .bitcast(I32),
+                in_=high_codes[32 * b : 32 * (b + 1), :].bitcast(I32).rearrange("p (l m) -> p l m", l=PER_GROUP),
+            )
 
-        page_bf.append(sb.tile([P, 4 * T2], BF16, name="page_bf1", tag="big", align_bytes=64))
         x_t = [
-            sb.tile([P, 4 * 512], BF16, name="x_t0", tag="raw3", align_bytes=64),
-            sb.tile([P, 4 * 512], BF16, name="x_t1", tag="x_t1"),
+            sb.tile([P, 4 * PICKS], BF16, name="x_t0", tag="raw3", align_bytes=64),
+            sb.tile([P, 4 * PICKS], BF16, name="x_t1", tag="big", align_bytes=64),
         ]
         x_bf = [sb.tile([P, 4 * PICKS], BF16, name=f"x_bf{g}", tag=f"raw{1 + g}", align_bytes=64) for g in range(GROUPS)]
-        picked = [raw[0][:, BANK : 2 * BANK], raw[0][:, 2 * BANK :], wgs_sb[:, :BANK], wgs_sb[:, BANK:]]
+        last_inputs = [h_half(SLICES - 1, 0), h_half(SLICES - 1, 1), wgs_sb[:, :HALF], wgs_sb[:, HALF:]]
+        picked = [last_inputs[i % PER_GROUP] for i in range(SLICES)]
 
-        def pick(i):
-            nc.vector.tensor_copy(out=picked[i % 4], in_=page[i][:].indirect(idx3[:]))
-
-        def cap_pick(i):
-            nc.vector.tensor_scalar(
-                out=picked[i % 4], in0=picked[i % 4], scalar1=caps[:, i : i + 1],
-                scalar2=None, op0=ALU.min,
+        def pick(i, first=0, count=PICKS):
+            nc.vector.tensor_copy(
+                out=picked[i][:, first : first + count],
+                in_=page[i][:].indirect(idx3[:, first // 16 : (first + count) // 16]),
             )
+
+        def cap_pick(i, first=0, count=PICKS):
+            part = picked[i][:, first : first + count]
+            nc.vector.tensor_scalar(out=part, in0=part, scalar1=caps[:, i : i + 1], scalar2=None, op0=ALU.min)
 
         def quantize_x(g):
             nc.vector.quantize_mx(out=x_codes[g][:].bitcast(FP8X4), scales=x_sc[g][:], in_=x_bf[g][:])
@@ -329,45 +367,57 @@ def tile_list_cork_taint_page_kernel(
                     lhsT_scale=w4_sc[:, first : first + P],
                     rhs=x_codes[g][:].bitcast(FP8X4),
                     rhs_scale=x_sc[g][:],
-                    start=(g == 0),
-                    stop=(g == GROUPS - 1),
+                    start=(g == GROUPS - 1),
+                    stop=(g == 0),
                 )
 
-        ring = []
+        def turn_x_back(g, job):
+            cols = slice(BACK * job, BACK * (job + 1))
+            turn_back(x_t[g][:, cols], x_bf[g][:, cols], next_bank(SLICES))
 
-        def ring_bank():
-            ring.append(banks[(len(ring) + 2) % 4])
-            return ring[-1]
-
-        pick(0)
-        for i in range(SLICES):
-            if i + 1 < SLICES:
-                pick(i + 1)
+        order = list(range(PER_GROUP, SLICES)) + list(range(PER_GROUP))
+        last = order[-1]
+        half_picks = PICKS // 2
+        pick(order[0])
+        for n, i in enumerate(order[:-1]):
+            if order[n + 1] == last:
+                quantize_x(1)
+                multiply_w4(1)
+                last_pick = sb.tile([P, PICKS], F32, name="last_pick", tag="raw2", align_bytes=64)
+                picked[last] = last_pick[:]
+                pick(last, 0, half_picks)
+            else:
+                pick(order[n + 1])
             cap_pick(i)
-            if i < 4:
-                quantize_page(0, i)
-            if i >= 1:
-                turn_page_back(1, i - 1, ring_bank())
-            turn(picked[i % 4], x_t[i // 4][:], i % 4, ring_bank())
-            if i == 3:
-                store_codes(0, 0, T2)
-                store_scales(0)
-            if i == 4:
-                for job in range(2):
-                    turn_back(x_t[0][:, 1024 * job : 1024 * (job + 1)], x_bf[0][:, 1024 * job : 1024 * (job + 1)], ring_bank())
-        turn_page_back(1, 7, ring_bank())
+            turn(picked[i], x_t[i // PER_GROUP][:], i % PER_GROUP, next_bank(SLICES))
+            if i == SLICES - 1:
+                turn_x_back(1, 0)
+                turn_x_back(1, 1)
+                used[SLICES] = used[SLICES] + 2
+        cap_pick(last, 0, half_picks)
+        pick(last, half_picks, half_picks)
+        cap_pick(last, half_picks, half_picks)
         for job in range(2):
-            turn_back(x_t[1][:, 1024 * job : 1024 * (job + 1)], x_bf[1][:, 1024 * job : 1024 * (job + 1)], ring_bank())
-        for c in range(3):
-            quantize_page(1, c)
-            store_codes(1, 512 * c, 512)
+            turn(
+                picked[last][:, half_picks * job : half_picks * (job + 1)],
+                x_t[0][:, BACK * job : BACK * (job + 1)], last % PER_GROUP, next_bank(SLICES),
+            )
+            turn_x_back(0, job)
+
+        low_codes = sb.tile([P, T2], U32, name="low_codes", tag=f"page{last}", align_bytes=64)
+        for c in range(T2 // CHUNK):
+            cols = slice(CHUNK * c, CHUNK * (c + 1))
+            nc.vector.quantize_mx(
+                out=low_codes[:, cols].bitcast(FP8X4), scales=low_sc[:, cols],
+                in_=group_bf[:, 4 * CHUNK * c : 4 * CHUNK * (c + 1)],
+            )
+        nc.sync.dma_start(out=out_2[0].rearrange("p m t -> p (m t)").bitcast(I32), in_=low_codes[:].bitcast(I32))
+        for q in range(4):
+            nc.sync.dma_start(
+                out=out_3[0, 4 * q : 4 * q + 4, :].bitcast(I32), in_=low_sc[32 * q : 32 * q + 4, :].bitcast(I32)
+            )
         quantize_x(0)
         multiply_w4(0)
-        quantize_x(1)
-        multiply_w4(1)
-        quantize_page(1, 3)
-        store_codes(1, 512 * 3, 512)
-        store_scales(1)
         for t in range(N // P):
             nc.vector.tensor_tensor(y_sb[:, t, :], banks[4 + t][:], y_sb[:, t, :], ALU.subtract)
             nc.sync.dma_start(out=out_0[P * t : P * (t + 1), :], in_=y_sb[:, t, :])

from contextlib import ExitStack

import concourse.mybir as mybir
from concourse.masks import make_identity

K, H, N, T, S, T2, PICKS = 1536, 1024, 512, 2048, 1024, 2048, 512
FLOPS = 2 * K * H * S + 2 * H * N * PICKS

F32 = mybir.dt.float32
BF16 = mybir.dt.bfloat16
I32 = mybir.dt.int32
U32 = mybir.dt.uint32
U16 = mybir.dt.uint16
U8 = mybir.dt.uint8
FP8X4 = mybir.dt.float8_e4m3fn_x4
FP4X4 = mybir.dt.float4_e2m1fn_x4
ACT = mybir.ActivationFunctionType
ALU = mybir.AluOpType

P = 128
PASS = 4 * P
BANK = 512
K_PASSES = K // PASS
SLICES = H // P
GROUPS = H // PASS
PER_GROUP = SLICES // GROUPS
RAW = K_PASSES * PASS
HALF = S // 2
QUARTER = S // 4
CHUNK = T2 // 4
BACK = 2 * PASS
W_TILES = 3
HALVED = 3
LOW_BACK_JOBS = ((0, 2), (2, 5), (5, 8))


def tile_list_cork_taint_page_kernel(
    tc, tab_words, tab_scales, offs, w1, b1, gain, page0, wgs, offs2, offs3, cap,
    w4_words, w4_scales, solvent, out_0, out_1, out_2, out_3,
):
    nc = tc.nc
    with ExitStack() as ctx:
        sb = ctx.enter_context(tc.tile_pool(name="sb", bufs=1))
        ps = ctx.enter_context(tc.psum_pool(name="ps", bufs=1))

        banks = [ps.tile([P, BANK], F32, name=f"bank{b}") for b in range(8)]

        idx = sb.tile([P, S // 16], U16, name="idx")
        idx2 = sb.tile([P, S // 16], U16, name="idx2")
        idx3 = sb.tile([P, PICKS // 16], U16, name="idx3")
        tab_sc = sb.tile([P, T], U8, name="tab_sc", align_bytes=64)
        tab_w = sb.tile([P, K_PASSES * T], I32, name="tab_w", tag="big", align_bytes=64)
        got_w = sb.tile([P, K_PASSES * S], U32, name="got_w", align_bytes=64)
        got_sc = sb.tile([P, S], U8, name="got_sc", align_bytes=64)
        raw_low = [sb.tile([P, RAW], F32, name=f"raw{i}", tag=f"raw{i}", align_bytes=64) for i in range(PER_GROUP)]
        w_bf = [sb.tile([P, RAW], BF16, name=f"w_bf{i}", align_bytes=64) for i in range(W_TILES)]
        w_codes = [sb.tile([P, K_PASSES * P], U32, name=f"w_codes{i}", align_bytes=64) for i in range(W_TILES)]
        w_sc = [sb.tile([P, K_PASSES * P], U8, name=f"w_sc{i}", align_bytes=64) for i in range(W_TILES)]
        page = [sb.tile([P, T2], F32, name=f"page{i}", tag=f"page{i}", align_bytes=64) for i in range(SLICES)]
        wgs_sb = sb.tile([P, S], F32, name="wgs_sb")
        ident = sb.tile([P, P], F32, name="ident")
        vec_rows = sb.tile([P, P], F32, name="vec_rows")
        vec_in = sb.tile([2 * SLICES, P], F32, name="vec_in")
        cap_rows = sb.tile([P, P], F32, name="cap_rows")
        vecs = sb.tile([P, 2 * SLICES], F32, name="vecs")
        caps = sb.tile([P, SLICES], F32, name="caps")
        wg_single = [sb.tile([P, S], F32, name=f"wg{i}", tag=f"wg{i}", align_bytes=64) for i in range(SLICES - 3)]
        wg_pair = sb.tile([P, 2 * S], F32, name="wg_pair", tag="wg_pair", align_bytes=64)
        wg = wg_single + [wg_pair[:, :S], wg_pair[:, S:], wgs_sb]
        group_t = [sb.tile([P, T2], BF16, name=f"group_t{c}") for c in range(T2 // CHUNK)]
        slice_bf = [sb.tile([P, T2], BF16, name=f"slice_bf{i}", align_bytes=64) for i in range(2)]
        high_sc = sb.tile([P, T2], U8, name="high_sc", align_bytes=64)
        low_sc = sb.tile([P, T2], U8, name="low_sc", align_bytes=64)
        x_codes = [sb.tile([P, PICKS], U32, name=f"x_codes{g}", align_bytes=64) for g in range(GROUPS)]
        x_sc = [sb.tile([P, PICKS], U8, name=f"x_sc{g}", align_bytes=64) for g in range(GROUPS)]
        w4_w = sb.tile([P, GROUPS * 2 * N], U8, name="w4_w", align_bytes=64)
        w4_sc = sb.tile([P, GROUPS * N], U8, name="w4_sc", align_bytes=64)
        y_sb = sb.tile([P, N // P, PICKS], F32, name="y_sb")

        raw = [t[:] for t in raw_low]

        def load_w1(i):
            for a in range(K_PASSES):
                nc.sync.dma_start(
                    out=raw[i][:, PASS * a : PASS * (a + 1)].rearrange("p (j c) -> p j c", j=4),
                    in_=w1[PASS * a : PASS * (a + 1), P * i : P * (i + 1)].rearrange("(p j) c -> p j c", j=4),
                )

        def load_words(a):
            nc.sync.dma_start(
                out=tab_w[:, T * a : T * (a + 1)],
                in_=tab_words[a].rearrange("p t i -> p (t i)").bitcast(I32),
            )

        def load_page(i):
            nc.sync.dma_start(out=page[i][:], in_=page0[P * i : P * (i + 1), :])

        nc.gpsimd.memset(tab_sc[:].bitcast(I32), 0)
        nc.gpsimd.memset(vec_rows[:], 0.0)
        make_identity(nc, ident[:])
        nc.gpsimd.memset(cap_rows[:], 0.0)
        nc.gpsimd.memset(w4_sc[:].bitcast(I32), 0)

        nc.sync.dma_start(idx[:], offs)
        load_words(0)
        for v, vec in enumerate((gain, b1)):
            nc.sync.dma_start(out=vec_in[SLICES * v : SLICES * (v + 1), :], in_=vec.rearrange("(i p) -> i p", p=P))
        for q in range(4):
            nc.scalar.dma_start(
                out=tab_sc[32 * q : 32 * q + 4 * K_PASSES, :].bitcast(I32),
                in_=tab_scales[:, 4 * q : 4 * q + 4, :].bitcast(I32),
            )
        nc.sync.dma_start(out=wgs_sb[:], in_=wgs)
        load_words(1)
        load_w1(0)
        load_words(2)
        load_page(0)
        nc.sync.dma_start(idx2[:], offs2)
        load_w1(1)
        nc.sync.dma_start(out=cap_rows[:SLICES, :], in_=cap.rearrange("(i p) -> i p", p=P))
        load_page(1)
        load_w1(2)
        load_w1(3)
        load_page(2)

        nc.gpsimd.tensor_copy(out=vec_rows[: 2 * SLICES, :], in_=vec_in[:])
        nc.tensor.transpose(banks[7][:, :P], vec_rows[:], ident[:])
        nc.scalar.copy(out=vecs[:], in_=banks[7][:, : 2 * SLICES])

        def weigh(i):
            nc.scalar.activation(out=wg[i][:], in_=wgs_sb[:], func=ACT.Copy, scale=vecs[:, i : i + 1])

        def quantize_w1(i):
            staged, codes, scales = w_bf[i % W_TILES], w_codes[i % W_TILES], w_sc[i % W_TILES]
            for a in range(K_PASSES):
                cols = slice(PASS * a, PASS * (a + 1))
                nc.scalar.copy(
                    out=staged[:, cols].rearrange("p (c n j) -> p c j n", n=4, j=4),
                    in_=raw[i][:, cols].rearrange("p (j c n) -> p c j n", n=4, j=4),
                )
            for first, last in ((0, 1), (1, 2), (2, 3)) if i == 0 else ((0, 2), (2, 3)):
                nc.vector.quantize_mx(
                    out=codes[:, P * first : P * last].bitcast(FP8X4),
                    scales=scales[:, P * first : P * last],
                    in_=staged[:, PASS * first : PASS * last],
                )

        def gather_words(a, first, count):
            nc.vector.tensor_copy(
                out=got_w[:, S * a + first : S * a + first + count],
                in_=tab_w[:, T * a : T * (a + 1)].bitcast(U32).indirect(idx[:, first // 16 : (first + count) // 16]),
            )

        gather_words(0, 0, S)
        nc.vector.tensor_copy(out=got_sc[:], in_=tab_sc[:].indirect(idx[:]))
        weigh(0)
        gather_words(1, 0, HALF)
        quantize_w1(0)
        gather_words(2, 0, HALF)
        gather_words(1, HALF, HALF)
        gather_words(2, HALF, HALF)

        raw_high = sb.tile([P, PER_GROUP * RAW], F32, name="raw_high", tag="big", align_bytes=64)
        raw.extend(raw_high[:, RAW * i : RAW * (i + 1)] for i in range(PER_GROUP))
        load_w1(PER_GROUP)
        for i in range(PER_GROUP + 1, SLICES):
            load_w1(i)
            load_page(i - 2)
        for i in range(SLICES - 2, SLICES):
            load_page(i)
        nc.sync.dma_start(idx3[:], offs3)
        nc.sync.dma_start(out=y_sb[:], in_=solvent.rearrange("(t p) j -> p t j", p=P))
        nc.sync.dma_start(
            out=w4_w[:].bitcast(I32).rearrange("p (g c) -> p g c", g=GROUPS),
            in_=w4_words.bitcast(I32).rearrange("g p c -> p g c"),
        )
        for q in range(4):
            nc.sync.dma_start(
                out=w4_sc[32 * q : 32 * q + 4, :].bitcast(I32).rearrange("r (g c) -> r g c", g=GROUPS),
                in_=w4_scales[:, 4 * q : 4 * q + 4, :].bitcast(I32).rearrange("g r c -> r g c"),
            )

        def feature_banks(i):
            return banks[4 * (i % 2) : 4 * (i % 2) + 4]

        def h_home(i):
            return i + 2 if i + 2 < SLICES else SLICES - 1 - i

        def h_half(i, half):
            if i < HALVED:
                home, third = ((0, 0), (1, 0), (1, 1), (2, 0), (3, 0), (4, 0))[2 * i + half]
            else:
                home, third = h_home(i), 1 + half
            return raw[home][:, HALF * third : HALF * (third + 1)]

        def multiply_w1(i):
            codes, scales = w_codes[i % W_TILES], w_sc[i % W_TILES]
            for quarter in range(4):
                first = QUARTER * quarter
                for a in range(K_PASSES):
                    nc.tensor.matmul_mx(
                        out=feature_banks(i)[quarter][:, :QUARTER],
                        lhsT=codes[:, P * a : P * (a + 1)].bitcast(FP8X4),
                        lhsT_scale=scales[:, P * a : P * (a + 1)],
                        rhs=got_w[:, S * a + first : S * a + first + QUARTER].bitcast(FP8X4),
                        rhs_scale=got_sc[4 * a : P, first : first + QUARTER],
                        start=(a == 0),
                        stop=(a == K_PASSES - 1),
                    )

        def activate(i, halves):
            for half in halves:
                for part in range(2):
                    nc.scalar.activation(
                        out=h_half(i, half)[:, QUARTER * part : QUARTER * (part + 1)],
                        in_=feature_banks(i)[2 * half + part][:, :QUARTER],
                        func=ACT.Silu,
                        bias=vecs[:, SLICES + i : SLICES + i + 1],
                    )

        def scatter_half(i, half):
            nc.vector.tensor_tensor(
                page[i][:].indirect(idx2[:, HALF // 16 * half : HALF // 16 * (half + 1)]),
                h_half(i, half), wg[i][:, HALF * half : HALF * (half + 1)], ALU.mult,
            )

        def scatter_whole(i):
            nc.vector.tensor_tensor(page[i][:].indirect(idx2[:]), raw[h_home(i)][:, HALF:], wg[i][:], ALU.mult)

        def turn(src, dst, place, bank):
            blocks = src.shape[1] // P
            for b in range(blocks):
                nc.tensor.transpose(bank[:, P * b : P * (b + 1)], src[:, P * b : P * (b + 1)], ident[:])
            nc.scalar.copy(
                out=dst.rearrange("m (b u l p e) -> m b u l p e", b=blocks, u=2, l=PER_GROUP, e=2)[:, :, :, place],
                in_=bank[:, : P * blocks].rearrange("m (b p u e) -> m b u p e", b=blocks, u=2, e=2),
            )

        def turn_back(src, dst, bank):
            words = src.bitcast(F32)
            for k in range(4):
                nc.tensor.transpose(bank[:, P * k : P * (k + 1)], words[:, P * k : P * (k + 1)], ident[:])
            nc.scalar.copy(
                out=dst.bitcast(F32).rearrange("p (b m u) -> p b m u", b=2, u=2),
                in_=bank[:].rearrange("p (b u m) -> p b m u", b=2, u=2),
            )

        used = [0] * (SLICES + 1)

        def next_bank(i):
            used[i] = used[i] + 1
            return feature_banks(i)[-used[i] % 4]

        def turn_low(i):
            for c in range(T2 // CHUNK):
                turn(page[i][:, CHUNK * c : CHUNK * (c + 1)], group_t[c][:], i, next_bank(i + 1))

        def turn_low_back(job, bank):
            turn_back(
                group_t[job // 2][:, BACK * (job % 2) : BACK * (job % 2 + 1)],
                group_bf[:, BACK * job : BACK * (job + 1)], bank,
            )

        def turn_high(i):
            halves = [
                sb.tile([P, BACK], BF16, name=f"slice_t{i}_{h}", tag=f"wg{2 * (i % 2) + h}", align_bytes=64)
                for h in range(2)
            ]
            for s in range(CHUNK // P):
                bank = next_bank(i + 1)
                for b in range(T2 // CHUNK):
                    first = CHUNK * b + P * s
                    nc.tensor.transpose(bank[:, P * b : P * (b + 1)], page[i][:, first : first + P], ident[:])
                nc.scalar.copy(
                    out=halves[s // 2][:, PASS * (s % 2) : PASS * (s % 2 + 1)].rearrange("m (u w e) -> m u w e", u=2, e=2),
                    in_=bank[:].rearrange("m (w u e) -> m u w e", u=2, e=2),
                )
            for job in range(2):
                turn_back(halves[job][:], slice_bf[i % 2][:, BACK * job : BACK * (job + 1)], next_bank(i + 1))

        def quantize_high(i):
            cols = slice(CHUNK * (i % PER_GROUP), CHUNK * (i % PER_GROUP + 1))
            nc.vector.quantize_mx(out=high_codes[:, cols].bitcast(FP8X4), scales=high_sc[:, cols], in_=slice_bf[i % 2][:])

        multiply_w1(0)
        for i in range(SLICES):
            if i < HALVED:
                if i == HALVED - 1:
                    quantize_w1(i + 1)
                activate(i, (0,))
                scatter_half(i, 0)
                quantize_w1(i + 2 if i == HALVED - 1 else i + 1)
                activate(i, (1,))
                scatter_half(i, 1)
            else:
                if i + 2 < SLICES:
                    quantize_w1(i + 2)
                    activate(i, (0, 1))
                scatter_whole(i)
            if i == 0:
                for later in range(1, SLICES):
                    weigh(later)
            if i + 1 < SLICES:
                multiply_w1(i + 1)
            if i + 1 < SLICES <= i + 3:
                activate(i + 1, (0, 1))
            nc.sync.dma_start(out=out_1[P * i : P * (i + 1), :], in_=page[i][:])
            if 1 <= i <= PER_GROUP:
                turn_low(i - 1)
            if i == PER_GROUP:
                bank = next_bank(i)
                nc.tensor.transpose(bank[:, :P], cap_rows[:], ident[:])
                nc.scalar.copy(out=caps[:], in_=bank[:, :SLICES])
            if i == PER_GROUP + 1:
                group_bf = sb.tile([P, 4 * T2], BF16, name="group_bf", tag=f"wg{PER_GROUP}", align_bytes=64)
            if i == PER_GROUP + 2:
                high_codes = sb.tile([P, T2], U32, name="high_codes", tag="wg_pair", align_bytes=64)
                quantize_high(PER_GROUP)
            if i > PER_GROUP:
                turn_high(i - 1)
                if i >= PER_GROUP + 2:
                    quantize_high(i - 1)
                for job in range(*LOW_BACK_JOBS[i - PER_GROUP - 1]):
                    turn_low_back(job, next_bank(i))
        turn_high(SLICES - 1)
        quantize_high(SLICES - 1)
        for b in range(4):
            nc.sync.dma_start(
                out=out_3[1, :, CHUNK * b : CHUNK * (b + 1)].rearrange("(l q) m -> q l m", l=PER_GROUP).bitcast(I32),
                in_=high_sc[32 * b : 32 * b + 4, :].bitcast(I32).rearrange("q (l m) -> q l m", l=PER_GROUP),
            )
        for b in (0, 2, 1, 3):
            nc.sync.dma_start(
                out=out_2[1, :, CHUNK * b : CHUNK * (b + 1), :]
                .rearrange("(l p) m t -> p l (m t)", l=PER_GROUP)
                .bitcast(I32),
                in_=high_codes[32 * b : 32 * (b + 1), :].bitcast(I32).rearrange("p (l m) -> p l m", l=PER_GROUP),
            )

        x_t = [
            sb.tile([P, 4 * PICKS], BF16, name="x_t0", tag="raw3", align_bytes=64),
            sb.tile([P, 4 * PICKS], BF16, name="x_t1", tag="big", align_bytes=64),
        ]
        x_bf = [sb.tile([P, 4 * PICKS], BF16, name=f"x_bf{g}", tag=f"raw{1 + g}", align_bytes=64) for g in range(GROUPS)]
        last_inputs = [h_half(SLICES - 1, 0), h_half(SLICES - 1, 1), wgs_sb[:, :HALF], wgs_sb[:, HALF:]]
        picked = [last_inputs[i % PER_GROUP] for i in range(SLICES)]

        def pick(i, first=0, count=PICKS):
            nc.vector.tensor_copy(
                out=picked[i][:, first : first + count],
                in_=page[i][:].indirect(idx3[:, first // 16 : (first + count) // 16]),
            )

        def cap_pick(i, first=0, count=PICKS):
            part = picked[i][:, first : first + count]
            nc.vector.tensor_scalar(out=part, in0=part, scalar1=caps[:, i : i + 1], scalar2=None, op0=ALU.min)

        def quantize_x(g):
            nc.vector.quantize_mx(out=x_codes[g][:].bitcast(FP8X4), scales=x_sc[g][:], in_=x_bf[g][:])

        def multiply_w4(g):
            for t in range(N // P):
                first = N * g + P * t
                nc.tensor.matmul_mx(
                    out=banks[4 + t][:],
                    lhsT=w4_w[:, 2 * first : 2 * (first + P)].bitcast(FP4X4),
                    lhsT_scale=w4_sc[:, first : first + P],
                    rhs=x_codes[g][:].bitcast(FP8X4),
                    rhs_scale=x_sc[g][:],
                    start=(g == GROUPS - 1),
                    stop=(g == 0),
                )

        def turn_x_back(g, job):
            cols = slice(BACK * job, BACK * (job + 1))
            turn_back(x_t[g][:, cols], x_bf[g][:, cols], next_bank(SLICES))

        order = list(range(PER_GROUP, SLICES)) + list(range(PER_GROUP))
        last = order[-1]
        half_picks = PICKS // 2
        pick(order[0])
        for n, i in enumerate(order[:-1]):
            if order[n + 1] == last:
                quantize_x(1)
                multiply_w4(1)
                last_pick = sb.tile([P, PICKS], F32, name="last_pick", tag="raw2", align_bytes=64)
                picked[last] = last_pick[:]
                pick(last, 0, half_picks)
            else:
                pick(order[n + 1])
            cap_pick(i)
            turn(picked[i], x_t[i // PER_GROUP][:], i % PER_GROUP, next_bank(SLICES))
            if i == SLICES - 1:
                turn_x_back(1, 0)
                turn_x_back(1, 1)
                used[SLICES] = used[SLICES] + 2
        cap_pick(last, 0, half_picks)
        pick(last, half_picks, half_picks)
        cap_pick(last, half_picks, half_picks)
        for job in range(2):
            turn(
                picked[last][:, half_picks * job : half_picks * (job + 1)],
                x_t[0][:, BACK * job : BACK * (job + 1)], last % PER_GROUP, next_bank(SLICES),
            )
            turn_x_back(0, job)

        low_codes = sb.tile([P, T2], U32, name="low_codes", tag=f"page{last}", align_bytes=64)
        for c in range(T2 // CHUNK):
            cols = slice(CHUNK * c, CHUNK * (c + 1))
            nc.vector.quantize_mx(
                out=low_codes[:, cols].bitcast(FP8X4), scales=low_sc[:, cols],
                in_=group_bf[:, 4 * CHUNK * c : 4 * CHUNK * (c + 1)],
            )
        nc.sync.dma_start(out=out_2[0].rearrange("p m t -> p (m t)").bitcast(I32), in_=low_codes[:].bitcast(I32))
        for q in range(4):
            nc.sync.dma_start(
                out=out_3[0, 4 * q : 4 * q + 4, :].bitcast(I32), in_=low_sc[32 * q : 32 * q + 4, :].bitcast(I32)
            )
        quantize_x(0)
        multiply_w4(0)
        for t in range(N // P):
            nc.vector.tensor_tensor(y_sb[:, t, :], banks[4 + t][:], y_sb[:, t, :], ALU.subtract)
            nc.sync.dma_start(out=out_0[P * t : P * (t + 1), :], in_=y_sb[:, t, :])
